import numpy as np, ml_dtypes
CORES = [8,136,40,168]
N = 4
import mx_ref
NC, G = 512, 4
C, C2 = np.float32(0.019), np.float32(0.029)
CNT = [[128,128,128,128],[128,128,128,128],[128,128,128,128],[128,128,128,128]]
OFF = [[sum(c[:e]) for e in range(N + 1)] for c in CNT]
BF = ml_dtypes.bfloat16
def cut(t, i, w=512):
    return t[:, w * i:w * i + w]
def tile(rs):
    return np.stack(rs, axis=2).reshape(128, -1).astype(BF)
def layer(w, X):
    out = []
    for i in range(G):
        for t in range(len(X)):
            p = mx_ref.matmul(mx_ref.quantize(cut(w, len(X) * i + t)), X[t])
            z = p if t == 0 else z + p
        out.append(z)
    return out
def act(Z):
    return [np.maximum(z, 0) * C for z in Z]
def setup_inputs(rng):
    def f(*shape):
        return mx_ref.flush((rng.standard_normal(shape, dtype=np.float32) * np.exp2(rng.integers(-2, 3, shape[:-1] + (1,)))).astype(BF))
    return {"x": f(N, 128, 4 * NC), "w1": f(N, 128, G * 512), "w2": f(N, 128, G * 512), "w3": f(N, 128, 512)}
def setup_inputs_blocks(rng):
    d = setup_inputs(rng)
    for k in ("x", "w3"): d[k] = mx_ref.spread(d[k], rng, 4)
    for k in ("w1", "w2"): d[k] = mx_ref.spread(d[k], rng, 2)
    return d
def setup_inputs_wide(rng):
    d = setup_inputs(rng)
    for k in ("x", "w1", "w2", "w3"): d[k] = mx_ref.flush((d[k].astype(np.float32) * np.exp2(rng.integers(-4, 5, (N, 1, 1))).astype(np.float32)).astype(BF))
    return d
def setup_inputs_zeros(rng):
    d = setup_inputs(rng); v = d["x"].reshape(N, 128, -1, 4).copy()
    v[np.broadcast_to((rng.random((N, 1, v.shape[2], 1)) < 0.33), v.shape)] = 0
    d["x"] = v.reshape(d["x"].shape)
    return d
def act2(Z):
    return [np.maximum(z, 0) * C2 for z in Z]
def reference(x, w1, w2, w3):
    h = [tile(act(layer(w1[j], [mx_ref.quantize(x[j])]))) for j in range(N)]
    g = []
    for e in range(N):
        t = np.concatenate([h[j][:, 4 * OFF[j][e]:4 * OFF[j][e + 1]] for j in range(N)], axis=1)
        g.append(tile(act2(layer(w2[e], [mx_ref.quantize(t)]))))
    y = np.zeros((N, 128, NC), np.float32)
    for j in range(N):
        back = []
        for e in range(N):
            a = sum(CNT[i][e] for i in range(j))
            back.append(g[e][:, 4 * a:4 * a + 4 * CNT[j][e]])
        y[j] = mx_ref.matmul(mx_ref.quantize(w3[j]), mx_ref.quantize(np.concatenate(back, axis=1)))
    return {"y": y}

@@ -1,0 +1,223 @@
+from concourse.mybir import dt, AluOpType, ActivationFunctionType
+
+C1, C2 = 0.019, 0.029
+N, NC, G = 4, 512, 4
+W = 128
+BANK = 512
+
+SCRATCH = {
+    "xb": ("sbuf", [128, 4 * NC], "bfloat16"),
+    "w1b": ("sbuf", [128, G * 4 * W], "bfloat16"),
+    "w2b": ("sbuf", [128, G * 4 * W], "bfloat16"),
+    "w3b": ("sbuf", [128, 4 * W], "bfloat16"),
+    "h": ("sbuf", [128, 4 * NC], "bfloat16"),
+    "gt": ("sbuf", [128, 4 * NC], "bfloat16"),
+    "xq": ("sbuf", [128, NC], "float8_e4m3fn_x4"), "xs": ("sbuf", [128, NC], "uint8"),
+    "w1q": ("sbuf", [128, G * W], "float8_e4m3fn_x4"), "w1s": ("sbuf", [128, G * W], "uint8"),
+    "w2q": ("sbuf", [128, G * W], "float8_e4m3fn_x4"), "w2s": ("sbuf", [128, G * W], "uint8"),
+    "w3q": ("sbuf", [128, W], "float8_e4m3fn_x4"), "w3s": ("sbuf", [128, W], "uint8"),
+    "hq": ("sbuf", [128, NC], "float8_e4m3fn_x4"), "hs": ("sbuf", [128, NC], "uint8"),
+    "gq": ("sbuf", [128, NC], "float8_e4m3fn_x4"), "gs": ("sbuf", [128, NC], "uint8"),
+    "bq": ("sbuf", [128, NC], "float8_e4m3fn_x4"), "bs": ("sbuf", [128, NC], "uint8"),
+    "aq": ("sbuf", [128, NC], "float8_e4m3fn_x4"), "as_": ("sbuf", [128, NC], "uint8"),
+    "yb": ("sbuf", [128, NC], "float32"),
+    "ps": ("psum", [128, 8 * BANK], "float32"),
+}
+SEMAPHORES = (["ldx%d" % s for s in range(4)] + ["ldw1_%d" % i for i in range(3)] + ["ldw2_%d" % i for i in range(2)] + ["ldw3"]
+              + ["qx%d" % s for s in range(4)] + ["qw1_%d" % i for i in range(4)] + ["qw2_%d" % i for i in range(4)] + ["qw3"]
+              + ["mm%d_%d" % (k, b) for k in range(8) for b in range(4)] + ["my%d" % s for s in range(4)]
+              + ["ra%d" % k for k in range(8)] + ["rv%d" % k for k in range(8)] + ["qt%d" % k for k in range(8)]
+              + ["out%d" % s for s in range(1, 4)] + ["home%d" % s for s in range(1, 4)]
+              + ["cy%d" % s for s in range(4)] + ["left", "stored"])
+
+
+def rank_program(g, core, T, topo):
+    me = T.rank_of(core)
+    if me is None:
+        return
+    cnt = T.tables["CNT"]
+
+    def sem(name):
+        return T.sem[name]
+
+    def home(j, e):
+        a = sum(cnt[j][:e])
+        return a, a + cnt[j][e]
+
+    def there(j, e):
+        a = sum(cnt[i][e] for i in range(j))
+        return a, a + cnt[j][e]
+
+    to = [(me + s) % N for s in (1, 2, 3, 0)]
+    frm = [(me - s) % N for s in (0, 1, 2, 3)]
+
+    def load(q, buf, src, a, b, s):
+        q.dma_start(T[buf][:, a:b], src[:, a:b]).then_inc(sem(s), 16)
+
+    xr = [home(me, e) for e in to]
+    load(g.sync, "w1b", T.w1, 0, 1024, "ldw1_0")
+    load(g.scalar, "xb", T.x, 4 * xr[0][0], 4 * xr[0][1], "ldx0")
+    load(g.scalar, "w1b", T.w1, 1024, 1536, "ldw1_1")
+    load(g.sync, "w1b", T.w1, 1536, 2048, "ldw1_2")
+    load(g.sync, "xb", T.x, 4 * xr[1][0], 4 * xr[1][1], "ldx1")
+    load(g.scalar, "xb", T.x, 4 * xr[2][0], 4 * xr[2][1], "ldx2")
+    load(g.sync, "xb", T.x, 4 * xr[3][0], 4 * xr[3][1], "ldx3")
+    load(g.scalar, "w2b", T.w2, 0, 1024, "ldw2_0")
+    load(g.sync, "w2b", T.w2, 1024, 2048, "ldw2_1")
+    load(g.sync, "w3b", T.w3, 0, 512, "ldw3")
+
+    def quant(codes, scales, tile, a, b, s):
+        g.vector.quantize_mx(T[codes][:, a:b], T[scales][:, a:b], T[tile][:, 4 * a:4 * b]).then_inc(sem(s), 1)
+
+    def bank(k, b):
+        return 4 * (k % 2) + b
+
+    def psv(k, b, n):
+        c = BANK * bank(k, b)
+        return T.ps[:, c:c + n]
+
+    def span(k):
+        return home(me, to[k]) if k < 4 else there(frm[k - 4], me)
+
+    def products(k):
+        a, b = span(k)
+        if k >= 2:
+            g.tensor.wait_ge(sem("ra%d" % (k - 2)), 2)
+            g.tensor.wait_ge(sem("rv%d" % (k - 2)), 2)
+        if k < 4:
+            wq, ws, pre = T.w1q, T.w1s, "qw1_%d"
+            g.tensor.wait_ge(sem("qx%d" % k), 1)
+            mq, ms = T.xq[:, a:b], T.xs[:, a:b]
+        else:
+            wq, ws, pre = T.w2q, T.w2s, "qw2_%d"
+            if k == 4:
+                c, d = home(me, me)
+                g.tensor.wait_ge(sem("qt3"), 1)
+                mq, ms = T.hq[:, c:d], T.hs[:, c:d]
+            else:
+                g.tensor.wait_ge(sem("out%d" % (k - 4)), arrivals[0])
+                mq, ms = T.bq[:, a:b], T.bs[:, a:b]
+        for i in range(G):
+            if k % 4 == 0:
+                g.tensor.wait_ge(sem(pre % i), 1)
+            g.tensor.matmul_mx(psv(k, i, b - a), wq[:, W * i:W * i + W], ws[:, W * i:W * i + W], mq, ms,
+                               True, True).then_inc(sem("mm%d_%d" % (k, i)), 1)
+
+    def step_out(k, b):
+        lo, hi = span(k)
+        return (T.h if k < 4 else T.gt)[:, 4 * lo + b:4 * hi:4]
+
+    def steps_scalar(k):
+        lo, hi = span(k)
+        for b in (0, 2):
+            g.scalar.wait_ge(sem("mm%d_%d" % (k, b)), 1)
+            g.scalar.activation(step_out(k, b), psv(k, b, hi - lo), ActivationFunctionType.Relu,
+                                scale=C1 if k < 4 else C2).then_inc(sem("ra%d" % k), 1)
+
+    def steps_vector(k):
+        lo, hi = span(k)
+        for b in (1, 3):
+            g.vector.wait_ge(sem("mm%d_%d" % (k, b)), 1)
+            g.vector.tensor_scalar(step_out(k, b), psv(k, b, hi - lo), 0.0, C1 if k < 4 else C2,
+                                   AluOpType.max, AluOpType.mult).then_inc(sem("rv%d" % k), 1)
+        g.vector.wait_ge(sem("ra%d" % k), 2)
+        g.vector.wait_ge(sem("rv%d" % k), 2)
+        if k < 4:
+            quant("hq", "hs", "h", lo, hi, "qt%d" % k)
+        else:
+            quant("gq", "gs", "gt", lo, hi, "qt%d" % k)
+
+    left = [0]
+
+    def send(dst_rank, dq, ds, sq, ss, d, s, name):
+        dst = T.cores[dst_rank]
+        m = topo.mask(core, dst)
+        rid, pid = topo.addr(dst, core)
+        ne = bin(m).count("1")
+        g.remote_dma(T[dq][:, d[0]:d[1]].bitcast(dt.uint8), T[sq][:, s[0]:s[1]].bitcast(dt.uint8),
+                     sem(name), sem("left"), pid, rid, m)
+        g.remote_dma(T[ds][:, d[0]:d[1]], T[ss][:, s[0]:s[1]], sem(name), sem("left"), pid, rid, m)
+        left[0] += 2 * ne
+
+    arrivals = [2 * bin(topo.mask(T.cores[to[0]], core)).count("1")]
+
+    for s in (1, 2, 3):
+        e = to[s - 1]
+        g.wait_ge(sem("qt%d" % (s - 1)), 1)
+        send(e, "bq", "bs", "hq", "hs", there(me, e), home(me, e), "out%d" % s)
+    for s in (1, 2, 3):
+        j = frm[s]
+        g.wait_ge(sem("qt%d" % (4 + s)), 1)
+        send(j, "aq", "as_", "gq", "gs", home(j, me), there(j, me), "home%d" % s)
+    g.wait_ge(sem("left"), left[0])
+
+    for k in range(8):
+        products(k)
+    yruns = [me] + [to[s - 1] for s in (1, 2, 3)]
+    ybank = [(8, 0), (9, 0), (8, 1), (9, 1)]
+    for s in range(4):
+        a, b = home(me, yruns[s])
+        if s == 0:
+            c, d = there(me, me)
+            g.tensor.wait_ge(sem("ra6"), 2)
+            g.tensor.wait_ge(sem("rv6"), 2)
+            g.tensor.wait_ge(sem("qw3"), 1)
+            g.tensor.wait_ge(sem("qt4"), 1)
+            mq, ms = T.gq[:, c:d], T.gs[:, c:d]
+        else:
+            if s == 1:
+                g.tensor.wait_ge(sem("ra7"), 2)
+                g.tensor.wait_ge(sem("rv7"), 2)
+            g.tensor.wait_ge(sem("home%d" % s), arrivals[0])
+            mq, ms = T.aq[:, a:b], T.as_[:, a:b]
+        g.tensor.matmul_mx(psv(ybank[s][0], ybank[s][1], b - a), T.w3q[:], T.w3s[:], mq, ms, True, True).then_inc(sem("my%d" % s), 1)
+
+    v = g.vector
+
+    def qx(k):
+        v.wait_ge(sem("ldx%d" % k), 16)
+        quant("xq", "xs", "xb", xr[k][0], xr[k][1], "qx%d" % k)
+
+    def qw(layer, i):
+        quant("w%dq" % layer, "w%ds" % layer, "w%db" % layer, W * i, W * i + W, "qw%d_%d" % (layer, i))
+
+    qx(0)
+    v.wait_ge(sem("ldw1_0"), 16)
+    qw(1, 0)
+    qw(1, 1)
+    v.wait_ge(sem("ldw1_1"), 16)
+    qw(1, 2)
+    v.wait_ge(sem("ldw1_2"), 16)
+    qw(1, 3)
+    steps_vector(0)
+    qx(1)
+    qx(2)
+    steps_vector(1)
+    qx(3)
+    steps_vector(2)
+    steps_vector(3)
+    v.wait_ge(sem("ldw2_0"), 16)
+    qw(2, 0)
+    qw(2, 1)
+    v.wait_ge(sem("ldw2_1"), 16)
+    qw(2, 2)
+    qw(2, 3)
+    steps_vector(4)
+    v.wait_ge(sem("ldw3"), 16)
+    quant("w3q", "w3s", "w3b", 0, W, "qw3")
+    steps_vector(5)
+    steps_vector(6)
+    steps_vector(7)
+    for s in range(4):
+        a, b = home(me, yruns[s])
+        v.wait_ge(sem("my%d" % s), 1)
+        v.tensor_copy(T.yb[:, a:b], psv(ybank[s][0], ybank[s][1], b - a)).then_inc(sem("cy%d" % s), 1)
+
+    for k in range(8):
+        steps_scalar(k)
+
+    for s in range(4):
+        a, b = home(me, yruns[s])
+        g.sync.wait_ge(sem("cy%d" % s), 1)
+        g.sync.dma_start(T.y[:, a:b], T.yb[:, a:b]).then_inc(sem("stored"), 16)
+    g.sync.wait_ge(sem("stored"), 64)

@@ -5,6 +5,14 @@ N, NC, G = 4, 512, 4
 W = 128
 BANK = 512
 
+LOADS = [("sync", "x", 0, 1), ("sync", "w1", 0, 2), ("sync", "w1", 2, 3), ("sync", "w1", 3, 4), ("sync", "x", 1, 2), ("sync", "x", 2, 4),
+         ("sync", "w2", 0, 4), ("sync", "w3", 0, 1)]
+VECTOR = ("x0 w1.0 w1.1 w1.2 w1.3 s0.1 s0.3 q0 x1 x2 s1.1 s1.3 q1 s2.1 s2.3 q2 x3 w2.0 w2.1 w2.2 w2.3 s3.3 s5.1 s5.3 q5 "
+          "s6.2 s6.3 q6 s7.1 s7.3 q7 q3 w3 s4.1 s4.3 q4 y0").split()
+SCALAR = "s0.0 s0.2 s1.0 s1.2 s2.0 s2.2 s3.0 s3.1 s3.2 s5.0 s5.2 s6.0 s6.1 s7.0 s7.2 s4.0 s4.2 y1 y2 y3".split()
+TENSOR = "0 1 2 3 5 6 7 4 y1 y2 y0 y3".split()
+STORES = [("sync", 1, 2), ("sync", 0), ("scalar", 3)]
+
 SCRATCH = {
     "xb": ("sbuf", [128, 4 * NC], "bfloat16"),
     "w1b": ("sbuf", [128, G * 4 * W], "bfloat16"),
@@ -23,12 +31,11 @@ SCRATCH = {
     "yb": ("sbuf", [128, NC], "float32"),
     "ps": ("psum", [128, 8 * BANK], "float32"),
 }
-SEMAPHORES = (["ldx%d" % s for s in range(4)] + ["ldw1_%d" % i for i in range(3)] + ["ldw2_%d" % i for i in range(2)] + ["ldw3"]
-              + ["qx%d" % s for s in range(4)] + ["qw1_%d" % i for i in range(4)] + ["qw2_%d" % i for i in range(4)] + ["qw3"]
-              + ["mm%d_%d" % (k, b) for k in range(8) for b in range(4)] + ["my%d" % s for s in range(4)]
-              + ["ra%d" % k for k in range(8)] + ["rv%d" % k for k in range(8)] + ["qt%d" % k for k in range(8)]
-              + ["out%d" % s for s in range(1, 4)] + ["home%d" % s for s in range(1, 4)]
-              + ["cy%d" % s for s in range(4)] + ["left", "stored"])
+SEMAPHORES = (["ld%d" % s for s in range(len(LOADS))] + ["qx%d" % s for s in range(4)] + ["qw1_%d" % i for i in range(4)]
+              + ["qw2_%d" % i for i in range(4)] + ["qw3"] + ["mm%d_%d" % (k, b) for k in range(8) for b in range(4)]
+              + ["st%d_%d" % (k, b) for k in range(8) for b in range(4)] + ["qt%d" % k for k in range(8)]
+              + ["my%d" % s for s in range(4)] + ["cy%d" % s for s in range(4)]
+              + ["out%d" % s for s in range(3)] + ["home%d" % s for s in range(3)] + ["left", "stored"])
 
 
 def rank_program(g, core, T, topo):
@@ -48,84 +55,26 @@ def rank_program(g, core, T, topo):
         a = sum(cnt[i][e] for i in range(j))
         return a, a + cnt[j][e]
 
-    to = [(me + s) % N for s in (1, 2, 3, 0)]
-    frm = [(me - s) % N for s in (0, 1, 2, 3)]
+    peer = [me ^ 2, me ^ 3, me ^ 1, me]
 
-    def load(q, buf, src, a, b, s):
-        q.dma_start(T[buf][:, a:b], src[:, a:b]).then_inc(sem(s), 16)
+    queues = {"sync": g.sync, "scalar": g.scalar, "vector": g.vector, "tensor": g.tensor}
+    known = {}
 
-    xr = [home(me, e) for e in to]
-    load(g.sync, "w1b", T.w1, 0, 1024, "ldw1_0")
-    load(g.scalar, "xb", T.x, 4 * xr[0][0], 4 * xr[0][1], "ldx0")
-    load(g.scalar, "w1b", T.w1, 1024, 1536, "ldw1_1")
-    load(g.sync, "w1b", T.w1, 1536, 2048, "ldw1_2")
-    load(g.sync, "xb", T.x, 4 * xr[1][0], 4 * xr[1][1], "ldx1")
-    load(g.scalar, "xb", T.x, 4 * xr[2][0], 4 * xr[2][1], "ldx2")
-    load(g.sync, "xb", T.x, 4 * xr[3][0], 4 * xr[3][1], "ldx3")
-    load(g.scalar, "w2b", T.w2, 0, 1024, "ldw2_0")
-    load(g.sync, "w2b", T.w2, 1024, 2048, "ldw2_1")
-    load(g.sync, "w3b", T.w3, 0, 512, "ldw3")
+    def need(q, name, n):
+        if known.get((q, name), 0) < n:
+            queues[q].wait_ge(sem(name), n)
+            known[(q, name)] = n
 
-    def quant(codes, scales, tile, a, b, s):
-        g.vector.quantize_mx(T[codes][:, a:b], T[scales][:, a:b], T[tile][:, 4 * a:4 * b]).then_inc(sem(s), 1)
-
-    def bank(k, b):
-        return 4 * (k % 2) + b
-
-    def psv(k, b, n):
-        c = BANK * bank(k, b)
-        return T.ps[:, c:c + n]
-
-    def span(k):
-        return home(me, to[k]) if k < 4 else there(frm[k - 4], me)
-
-    def products(k):
-        a, b = span(k)
-        if k >= 2:
-            g.tensor.wait_ge(sem("ra%d" % (k - 2)), 2)
-            g.tensor.wait_ge(sem("rv%d" % (k - 2)), 2)
-        if k < 4:
-            wq, ws, pre = T.w1q, T.w1s, "qw1_%d"
-            g.tensor.wait_ge(sem("qx%d" % k), 1)
-            mq, ms = T.xq[:, a:b], T.xs[:, a:b]
+    have = {}
+    for n, (q, what, lo, hi) in enumerate(LOADS):
+        if what == "x":
+            rs = [home(me, peer[k]) for k in range(lo, hi)]
+            a, b = 4 * min(r[0] for r in rs), 4 * max(r[1] for r in rs)
         else:
-            wq, ws, pre = T.w2q, T.w2s, "qw2_%d"
-            if k == 4:
-                c, d = home(me, me)
-                g.tensor.wait_ge(sem("qt3"), 1)
-                mq, ms = T.hq[:, c:d], T.hs[:, c:d]
-            else:
-                g.tensor.wait_ge(sem("out%d" % (k - 4)), arrivals[0])
-                mq, ms = T.bq[:, a:b], T.bs[:, a:b]
-        for i in range(G):
-            if k % 4 == 0:
-                g.tensor.wait_ge(sem(pre % i), 1)
-            g.tensor.matmul_mx(psv(k, i, b - a), wq[:, W * i:W * i + W], ws[:, W * i:W * i + W], mq, ms,
-                               True, True).then_inc(sem("mm%d_%d" % (k, i)), 1)
-
-    def step_out(k, b):
-        lo, hi = span(k)
-        return (T.h if k < 4 else T.gt)[:, 4 * lo + b:4 * hi:4]
-
-    def steps_scalar(k):
-        lo, hi = span(k)
-        for b in (0, 2):
-            g.scalar.wait_ge(sem("mm%d_%d" % (k, b)), 1)
-            g.scalar.activation(step_out(k, b), psv(k, b, hi - lo), ActivationFunctionType.Relu,
-                                scale=C1 if k < 4 else C2).then_inc(sem("ra%d" % k), 1)
-
-    def steps_vector(k):
-        lo, hi = span(k)
-        for b in (1, 3):
-            g.vector.wait_ge(sem("mm%d_%d" % (k, b)), 1)
-            g.vector.tensor_scalar(step_out(k, b), psv(k, b, hi - lo), 0.0, C1 if k < 4 else C2,
-                                   AluOpType.max, AluOpType.mult).then_inc(sem("rv%d" % k), 1)
-        g.vector.wait_ge(sem("ra%d" % k), 2)
-        g.vector.wait_ge(sem("rv%d" % k), 2)
-        if k < 4:
-            quant("hq", "hs", "h", lo, hi, "qt%d" % k)
-        else:
-            quant("gq", "gs", "gt", lo, hi, "qt%d" % k)
+            a, b = 4 * W * lo, 4 * W * hi
+        queues[q].dma_start(T[what + "b"][:, a:b], T[what][:, a:b]).then_inc(sem("ld%d" % n), 16)
+        for k in range(lo, hi):
+            have[(what, k)] = "ld%d" % n
 
     left = [0]
 
@@ -133,91 +82,127 @@ def rank_program(g, core, T, topo):
         dst = T.cores[dst_rank]
         m = topo.mask(core, dst)
         rid, pid = topo.addr(dst, core)
-        ne = bin(m).count("1")
         g.remote_dma(T[dq][:, d[0]:d[1]].bitcast(dt.uint8), T[sq][:, s[0]:s[1]].bitcast(dt.uint8),
                      sem(name), sem("left"), pid, rid, m)
         g.remote_dma(T[ds][:, d[0]:d[1]], T[ss][:, s[0]:s[1]], sem(name), sem("left"), pid, rid, m)
-        left[0] += 2 * ne
+        left[0] += 2 * bin(m).count("1")
 
-    arrivals = [2 * bin(topo.mask(T.cores[to[0]], core)).count("1")]
+    arrive = [2 * bin(topo.mask(T.cores[peer[s]], core)).count("1") for s in range(3)]
 
-    for s in (1, 2, 3):
-        e = to[s - 1]
-        g.wait_ge(sem("qt%d" % (s - 1)), 1)
-        send(e, "bq", "bs", "hq", "hs", there(me, e), home(me, e), "out%d" % s)
-    for s in (1, 2, 3):
-        j = frm[s]
-        g.wait_ge(sem("qt%d" % (4 + s)), 1)
-        send(j, "aq", "as_", "gq", "gs", home(j, me), there(j, me), "home%d" % s)
+    for s in range(3):
+        g.wait_ge(sem("qt%d" % s), 1)
+        send(peer[s], "bq", "bs", "hq", "hs", there(me, peer[s]), home(me, peer[s]), "out%d" % s)
+    for s in range(3):
+        g.wait_ge(sem("qt%d" % (5 + s)), 1)
+        send(peer[s], "aq", "as_", "gq", "gs", home(peer[s], me), there(peer[s], me), "home%d" % s)
     g.wait_ge(sem("left"), left[0])
 
-    for k in range(8):
-        products(k)
-    yruns = [me] + [to[s - 1] for s in (1, 2, 3)]
-    ybank = [(8, 0), (9, 0), (8, 1), (9, 1)]
-    for s in range(4):
-        a, b = home(me, yruns[s])
-        if s == 0:
-            c, d = there(me, me)
-            g.tensor.wait_ge(sem("ra6"), 2)
-            g.tensor.wait_ge(sem("rv6"), 2)
-            g.tensor.wait_ge(sem("qw3"), 1)
-            g.tensor.wait_ge(sem("qt4"), 1)
-            mq, ms = T.gq[:, c:d], T.gs[:, c:d]
+    def span(k):
+        if k < 4:
+            return home(me, peer[k])
+        return there(peer[k - 5] if k > 4 else me, me)
+
+    bank = {}
+    reader = [None] * 8
+    turn = 0
+    for it in TENSOR:
+        if it[0] == "y":
+            s = int(it[1])
+            a, b = home(me, peer[s - 1] if s else me)
+            if s == 0:
+                c, d = there(me, me)
+                need("tensor", "qt4", 1)
+                mq, ms = T.gq[:, c:d], T.gs[:, c:d]
+            else:
+                need("tensor", "home%d" % (s - 1), arrive[s - 1])
+                mq, ms = T.aq[:, a:b], T.as_[:, a:b]
+            jobs = [(it, T.w3q[:], T.w3s[:], "my%d" % s, "qw3", "cy%d" % s)]
         else:
-            if s == 1:
-                g.tensor.wait_ge(sem("ra7"), 2)
-                g.tensor.wait_ge(sem("rv7"), 2)
-            g.tensor.wait_ge(sem("home%d" % s), arrivals[0])
-            mq, ms = T.aq[:, a:b], T.as_[:, a:b]
-        g.tensor.matmul_mx(psv(ybank[s][0], ybank[s][1], b - a), T.w3q[:], T.w3s[:], mq, ms, True, True).then_inc(sem("my%d" % s), 1)
+            k = int(it)
+            a, b = span(k)
+            if k < 4:
+                need("tensor", "qx%d" % k, 1)
+                mq, ms, wq, ws, pre = T.xq[:, a:b], T.xs[:, a:b], T.w1q, T.w1s, "qw1_%d"
+            else:
+                wq, ws, pre = T.w2q, T.w2s, "qw2_%d"
+                if k == 4:
+                    c, d = home(me, me)
+                    need("tensor", "qt3", 1)
+                    mq, ms = T.hq[:, c:d], T.hs[:, c:d]
+                else:
+                    need("tensor", "out%d" % (k - 5), arrive[k - 5])
+                    mq, ms = T.bq[:, a:b], T.bs[:, a:b]
+            jobs = [((k, i), wq[:, W * i:W * i + W], ws[:, W * i:W * i + W], "mm%d_%d" % (k, i), pre % i, "st%d_%d" % (k, i))
+                    for i in range(G)]
+        for name, wt, wt_s, done, packed, read in jobs:
+            c = turn % 8
+            turn += 1
+            bank[name] = BANK * c
+            if reader[c]:
+                need("tensor", reader[c], 1)
+            reader[c] = read
+            need("tensor", packed, 1)
+            g.tensor.matmul_mx(T.ps[:, BANK * c:BANK * c + b - a], wt, wt_s, mq, ms, True, True).then_inc(sem(done), 1)
 
-    v = g.vector
+    def quant(codes, scales, tile, a, b, s):
+        g.vector.quantize_mx(T[codes][:, a:b], T[scales][:, a:b], T[tile][:, 4 * a:4 * b]).then_inc(sem(s), 1)
 
-    def qx(k):
-        v.wait_ge(sem("ldx%d" % k), 16)
-        quant("xq", "xs", "xb", xr[k][0], xr[k][1], "qx%d" % k)
+    def run(q, it):
+        if it[0] == "x":
+            k = int(it[1])
+            a, b = home(me, peer[k])
+            need(q, have[("x", k)], 16)
+            quant("xq", "xs", "xb", a, b, "qx%d" % k)
+        elif it == "w3":
+            need(q, have[("w3", 0)], 16)
+            quant("w3q", "w3s", "w3b", 0, W, "qw3")
+        elif it[0] == "w":
+            w, i = it[:2], int(it[3])
+            need(q, have[(w, i)], 16)
+            quant(w + "q", w + "s", w + "b", W * i, W * i + W, "q%s_%d" % (w, i))
+        elif it[0] == "q":
+            k = int(it[1])
+            a, b = span(k)
+            for i in range(G):
+                need(q, "st%d_%d" % (k, i), 1)
+            if k < 4:
+                quant("hq", "hs", "h", a, b, "qt%d" % k)
+            else:
+                quant("gq", "gs", "gt", a, b, "qt%d" % k)
+        elif it[0] == "s":
+            k, i = int(it[1]), int(it[3])
+            a, b = span(k)
+            need(q, "mm%d_%d" % (k, i), 1)
+            out = (T.h if k < 4 else T.gt)[:, 4 * a + i:4 * b:4]
+            c = bank[(k, i)]
+            src = T.ps[:, c:c + b - a]
+            f = C1 if k < 4 else C2
+            if q == "scalar":
+                o = g.scalar.activation(out, src, ActivationFunctionType.Relu, scale=f)
+            else:
+                o = g.vector.tensor_scalar(out, src, 0.0, f, AluOpType.max, AluOpType.mult)
+            o.then_inc(sem("st%d_%d" % (k, i)), 1)
+        else:
+            s = int(it[1])
+            a, b = home(me, peer[s - 1] if s else me)
+            need(q, "my%d" % s, 1)
+            src = T.ps[:, bank[it]:bank[it] + b - a]
+            if q == "scalar":
+                o = g.scalar.activation(T.yb[:, a:b], src, ActivationFunctionType.Copy)
+            else:
+                o = g.vector.tensor_copy(T.yb[:, a:b], src)
+            o.then_inc(sem("cy%d" % s), 1)
 
-    def qw(layer, i):
-        quant("w%dq" % layer, "w%ds" % layer, "w%db" % layer, W * i, W * i + W, "qw%d_%d" % (layer, i))
+    for it in VECTOR:
+        run("vector", it)
+    for it in SCALAR:
+        run("scalar", it)
 
-    qx(0)
-    v.wait_ge(sem("ldw1_0"), 16)
-    qw(1, 0)
-    qw(1, 1)
-    v.wait_ge(sem("ldw1_1"), 16)
-    qw(1, 2)
-    v.wait_ge(sem("ldw1_2"), 16)
-    qw(1, 3)
-    steps_vector(0)
-    qx(1)
-    qx(2)
-    steps_vector(1)
-    qx(3)
-    steps_vector(2)
-    steps_vector(3)
-    v.wait_ge(sem("ldw2_0"), 16)
-    qw(2, 0)
-    qw(2, 1)
-    v.wait_ge(sem("ldw2_1"), 16)
-    qw(2, 2)
-    qw(2, 3)
-    steps_vector(4)
-    v.wait_ge(sem("ldw3"), 16)
-    quant("w3q", "w3s", "w3b", 0, W, "qw3")
-    steps_vector(5)
-    steps_vector(6)
-    steps_vector(7)
-    for s in range(4):
-        a, b = home(me, yruns[s])
-        v.wait_ge(sem("my%d" % s), 1)
-        v.tensor_copy(T.yb[:, a:b], psv(ybank[s][0], ybank[s][1], b - a)).then_inc(sem("cy%d" % s), 1)
-
-    for k in range(8):
-        steps_scalar(k)
-
-    for s in range(4):
-        a, b = home(me, yruns[s])
-        g.sync.wait_ge(sem("cy%d" % s), 1)
-        g.sync.dma_start(T.y[:, a:b], T.yb[:, a:b]).then_inc(sem("stored"), 16)
-    g.sync.wait_ge(sem("stored"), 64)
+    for st in STORES:
+        q = st[0]
+        rs = [home(me, peer[s - 1] if s else me) for s in st[1:]]
+        for s in st[1:]:
+            need(q, "cy%d" % s, 1)
+        a, b = min(r[0] for r in rs), max(r[1] for r in rs)
+        queues[q].dma_start(T.y[:, a:b], T.yb[:, a:b]).then_inc(sem("stored"), 16)
+    g.sync.wait_ge(sem("stored"), 16 * len(STORES))

from concourse.mybir import dt, AluOpType, ActivationFunctionType

C1, C2 = 0.019, 0.029
N, NC, G = 4, 512, 4
W = 128
BANK = 512

LOADS = [("sync", "x", 0, 1), ("sync", "w1", 0, 2), ("sync", "w1", 2, 3), ("sync", "w1", 3, 4), ("sync", "x", 1, 2), ("sync", "x", 2, 4),
         ("sync", "w2", 0, 4), ("sync", "w3", 0, 1)]
VECTOR = ("x0 w1.0 w1.1 w1.2 w1.3 s0.1 s0.3 q0 x1 x2 s1.1 s1.3 q1 s2.1 s2.3 q2 x3 w2.0 w2.1 w2.2 w2.3 s3.3 s5.1 s5.3 q5 "
          "s6.2 s6.3 q6 s7.1 s7.3 q7 q3 w3 s4.1 s4.3 q4 y0").split()
SCALAR = "s0.0 s0.2 s1.0 s1.2 s2.0 s2.2 s3.0 s3.1 s3.2 s5.0 s5.2 s6.0 s6.1 s7.0 s7.2 s4.0 s4.2 y1 y2 y3".split()
TENSOR = "0 1 2 3 5 6 7 4 y1 y2 y0 y3".split()
STORES = [("sync", 1, 2), ("sync", 0), ("scalar", 3)]

SCRATCH = {
    "xb": ("sbuf", [128, 4 * NC], "bfloat16"),
    "w1b": ("sbuf", [128, G * 4 * W], "bfloat16"),
    "w2b": ("sbuf", [128, G * 4 * W], "bfloat16"),
    "w3b": ("sbuf", [128, 4 * W], "bfloat16"),
    "h": ("sbuf", [128, 4 * NC], "bfloat16"),
    "gt": ("sbuf", [128, 4 * NC], "bfloat16"),
    "xq": ("sbuf", [128, NC], "float8_e4m3fn_x4"), "xs": ("sbuf", [128, NC], "uint8"),
    "w1q": ("sbuf", [128, G * W], "float8_e4m3fn_x4"), "w1s": ("sbuf", [128, G * W], "uint8"),
    "w2q": ("sbuf", [128, G * W], "float8_e4m3fn_x4"), "w2s": ("sbuf", [128, G * W], "uint8"),
    "w3q": ("sbuf", [128, W], "float8_e4m3fn_x4"), "w3s": ("sbuf", [128, W], "uint8"),
    "hq": ("sbuf", [128, NC], "float8_e4m3fn_x4"), "hs": ("sbuf", [128, NC], "uint8"),
    "gq": ("sbuf", [128, NC], "float8_e4m3fn_x4"), "gs": ("sbuf", [128, NC], "uint8"),
    "bq": ("sbuf", [128, NC], "float8_e4m3fn_x4"), "bs": ("sbuf", [128, NC], "uint8"),
    "aq": ("sbuf", [128, NC], "float8_e4m3fn_x4"), "as_": ("sbuf", [128, NC], "uint8"),
    "yb": ("sbuf", [128, NC], "float32"),
    "ps": ("psum", [128, 8 * BANK], "float32"),
}
SEMAPHORES = (["ld%d" % s for s in range(len(LOADS))] + ["qx%d" % s for s in range(4)] + ["qw1_%d" % i for i in range(4)]
              + ["qw2_%d" % i for i in range(4)] + ["qw3"] + ["mm%d_%d" % (k, b) for k in range(8) for b in range(4)]
              + ["st%d_%d" % (k, b) for k in range(8) for b in range(4)] + ["qt%d" % k for k in range(8)]
              + ["my%d" % s for s in range(4)] + ["cy%d" % s for s in range(4)]
              + ["out%d" % s for s in range(3)] + ["home%d" % s for s in range(3)] + ["left", "stored"])


def rank_program(g, core, T, topo):
    me = T.rank_of(core)
    if me is None:
        return
    cnt = T.tables["CNT"]

    def sem(name):
        return T.sem[name]

    def home(j, e):
        a = sum(cnt[j][:e])
        return a, a + cnt[j][e]

    def there(j, e):
        a = sum(cnt[i][e] for i in range(j))
        return a, a + cnt[j][e]

    peer = [me ^ 2, me ^ 3, me ^ 1, me]

    queues = {"sync": g.sync, "scalar": g.scalar, "vector": g.vector, "tensor": g.tensor}
    known = {}

    def need(q, name, n):
        if known.get((q, name), 0) < n:
            queues[q].wait_ge(sem(name), n)
            known[(q, name)] = n

    have = {}
    for n, (q, what, lo, hi) in enumerate(LOADS):
        if what == "x":
            rs = [home(me, peer[k]) for k in range(lo, hi)]
            a, b = 4 * min(r[0] for r in rs), 4 * max(r[1] for r in rs)
        else:
            a, b = 4 * W * lo, 4 * W * hi
        queues[q].dma_start(T[what + "b"][:, a:b], T[what][:, a:b]).then_inc(sem("ld%d" % n), 16)
        for k in range(lo, hi):
            have[(what, k)] = "ld%d" % n

    left = [0]

    def send(dst_rank, dq, ds, sq, ss, d, s, name):
        dst = T.cores[dst_rank]
        m = topo.mask(core, dst)
        rid, pid = topo.addr(dst, core)
        g.remote_dma(T[dq][:, d[0]:d[1]].bitcast(dt.uint8), T[sq][:, s[0]:s[1]].bitcast(dt.uint8),
                     sem(name), sem("left"), pid, rid, m)
        g.remote_dma(T[ds][:, d[0]:d[1]], T[ss][:, s[0]:s[1]], sem(name), sem("left"), pid, rid, m)
        left[0] += 2 * bin(m).count("1")

    arrive = [2 * bin(topo.mask(T.cores[peer[s]], core)).count("1") for s in range(3)]

    for s in range(3):
        g.wait_ge(sem("qt%d" % s), 1)
        send(peer[s], "bq", "bs", "hq", "hs", there(me, peer[s]), home(me, peer[s]), "out%d" % s)
    for s in range(3):
        g.wait_ge(sem("qt%d" % (5 + s)), 1)
        send(peer[s], "aq", "as_", "gq", "gs", home(peer[s], me), there(peer[s], me), "home%d" % s)
    g.wait_ge(sem("left"), left[0])

    def span(k):
        if k < 4:
            return home(me, peer[k])
        return there(peer[k - 5] if k > 4 else me, me)

    bank = {}
    reader = [None] * 8
    turn = 0
    for it in TENSOR:
        if it[0] == "y":
            s = int(it[1])
            a, b = home(me, peer[s - 1] if s else me)
            if s == 0:
                c, d = there(me, me)
                need("tensor", "qt4", 1)
                mq, ms = T.gq[:, c:d], T.gs[:, c:d]
            else:
                need("tensor", "home%d" % (s - 1), arrive[s - 1])
                mq, ms = T.aq[:, a:b], T.as_[:, a:b]
            jobs = [(it, T.w3q[:], T.w3s[:], "my%d" % s, "qw3", "cy%d" % s)]
        else:
            k = int(it)
            a, b = span(k)
            if k < 4:
                need("tensor", "qx%d" % k, 1)
                mq, ms, wq, ws, pre = T.xq[:, a:b], T.xs[:, a:b], T.w1q, T.w1s, "qw1_%d"
            else:
                wq, ws, pre = T.w2q, T.w2s, "qw2_%d"
                if k == 4:
                    c, d = home(me, me)
                    need("tensor", "qt3", 1)
                    mq, ms = T.hq[:, c:d], T.hs[:, c:d]
                else:
                    need("tensor", "out%d" % (k - 5), arrive[k - 5])
                    mq, ms = T.bq[:, a:b], T.bs[:, a:b]
            jobs = [((k, i), wq[:, W * i:W * i + W], ws[:, W * i:W * i + W], "mm%d_%d" % (k, i), pre % i, "st%d_%d" % (k, i))
                    for i in range(G)]
        for name, wt, wt_s, done, packed, read in jobs:
            c = turn % 8
            turn += 1
            bank[name] = BANK * c
            if reader[c]:
                need("tensor", reader[c], 1)
            reader[c] = read
            need("tensor", packed, 1)
            g.tensor.matmul_mx(T.ps[:, BANK * c:BANK * c + b - a], wt, wt_s, mq, ms, True, True).then_inc(sem(done), 1)

    def quant(codes, scales, tile, a, b, s):
        g.vector.quantize_mx(T[codes][:, a:b], T[scales][:, a:b], T[tile][:, 4 * a:4 * b]).then_inc(sem(s), 1)

    def run(q, it):
        if it[0] == "x":
            k = int(it[1])
            a, b = home(me, peer[k])
            need(q, have[("x", k)], 16)
            quant("xq", "xs", "xb", a, b, "qx%d" % k)
        elif it == "w3":
            need(q, have[("w3", 0)], 16)
            quant("w3q", "w3s", "w3b", 0, W, "qw3")
        elif it[0] == "w":
            w, i = it[:2], int(it[3])
            need(q, have[(w, i)], 16)
            quant(w + "q", w + "s", w + "b", W * i, W * i + W, "q%s_%d" % (w, i))
        elif it[0] == "q":
            k = int(it[1])
            a, b = span(k)
            for i in range(G):
                need(q, "st%d_%d" % (k, i), 1)
            if k < 4:
                quant("hq", "hs", "h", a, b, "qt%d" % k)
            else:
                quant("gq", "gs", "gt", a, b, "qt%d" % k)
        elif it[0] == "s":
            k, i = int(it[1]), int(it[3])
            a, b = span(k)
            need(q, "mm%d_%d" % (k, i), 1)
            out = (T.h if k < 4 else T.gt)[:, 4 * a + i:4 * b:4]
            c = bank[(k, i)]
            src = T.ps[:, c:c + b - a]
            f = C1 if k < 4 else C2
            if q == "scalar":
                o = g.scalar.activation(out, src, ActivationFunctionType.Relu, scale=f)
            else:
                o = g.vector.tensor_scalar(out, src, 0.0, f, AluOpType.max, AluOpType.mult)
            o.then_inc(sem("st%d_%d" % (k, i)), 1)
        else:
            s = int(it[1])
            a, b = home(me, peer[s - 1] if s else me)
            need(q, "my%d" % s, 1)
            src = T.ps[:, bank[it]:bank[it] + b - a]
            if q == "scalar":
                o = g.scalar.activation(T.yb[:, a:b], src, ActivationFunctionType.Copy)
            else:
                o = g.vector.tensor_copy(T.yb[:, a:b], src)
            o.then_inc(sem("cy%d" % s), 1)

    for it in VECTOR:
        run("vector", it)
    for it in SCALAR:
        run("scalar", it)

    for st in STORES:
        q = st[0]
        rs = [home(me, peer[s - 1] if s else me) for s in st[1:]]
        for s in st[1:]:
            need(q, "cy%d" % s, 1)
        a, b = min(r[0] for r in rs), max(r[1] for r in rs)
        queues[q].dma_start(T.y[:, a:b], T.yb[:, a:b]).then_inc(sem("stored"), 16)
    g.sync.wait_ge(sem("stored"), 16 * len(STORES))
